import numpy as np
import ml_dtypes


def mxq(x, axis, fmt="e4m3"):
    dtype, down = {"e4m3": (ml_dtypes.float8_e4m3fn, 7), "e5m2": (ml_dtypes.float8_e5m2, 14)}[fmt]
    v = np.moveaxis(np.asarray(x, np.float32).astype(ml_dtypes.bfloat16).astype(np.float64), axis, -1)
    blocks = v.reshape(v.shape[:-1] + (-1, 32))
    amax = np.abs(blocks).max(-1, keepdims=True)
    byte = np.maximum(np.where(amax > 0, np.frexp(amax)[1] - 1 + 127, 0) - down, 1)
    scale = np.exp2(byte - 127.0)
    codes = (blocks / scale).astype(np.float32).astype(dtype).astype(np.float64)
    return np.moveaxis((codes * scale).reshape(v.shape), -1, axis)


WIDE = False


def mx_kscale(k):
    if not WIDE:
        return np.ones(k)
    levels = np.array([10, -10, 5, -5, 0])
    if k % 512:
        return np.exp2(np.random.permutation(np.resize(levels, k // 32))).repeat(32)
    a = np.empty((k // 512, 16))
    for p in range(k // 512):
        a[p, :8] = np.random.permutation(np.resize(levels, 8))
        for g in range(8):
            far = levels[np.abs(levels - a[p, g]) >= 10]
            a[p, g + 8] = far[np.random.randint(len(far))]
    return np.exp2(a.ravel()).repeat(32)


def f64(x):
    return np.asarray(x).astype(np.float64)


def striped(idx):
    return np.tile(idx.reshape(-1, 16).T, (8, 1)).astype(np.uint16)


def unstriped(offs):
    return offs[:16].T.reshape(-1).astype(np.int64)


E2M1 = np.array([0.0, 0.5, 1.0, 1.5, 2.0, 3.0, 4.0, 6.0, -0.0, -0.5, -1.0, -1.5, -2.0, -3.0, -4.0, -6.0])


def pack_weight(w, fmt):
    k, n = w.shape
    w = f64(np.asarray(w, np.float32).astype(ml_dtypes.bfloat16)).reshape(k // 32, 32, n)
    amax = np.abs(w).max(1)
    if fmt == "e4m3":
        byte = np.frexp(amax)[1] - 1 + 127 - 7
    else:
        mant, ex = np.frexp(amax / 6.0)
        byte = np.where(mant > 0.5, ex, ex - 1) + 127
    byte = np.clip(np.where(amax > 0, byte, 1), 1, 254)
    scaled = (w * np.exp2(127.0 - byte)[:, None, :]).reshape(k, n).astype(np.float32)
    by_word = np.ascontiguousarray(scaled.reshape(k // 512, 128, 4, n).transpose(0, 1, 3, 2))
    if fmt == "e4m3":
        words = by_word.astype(ml_dtypes.float8_e4m3fn).view(np.uint8)
    else:
        c = by_word.astype(ml_dtypes.float4_e2m1fn).view(np.uint8) & 0xF
        words = (c[..., 0::2] | (c[..., 1::2] << 4)).reshape(k // 512, 128, 2 * n)
    return np.ascontiguousarray(words), np.ascontiguousarray(byte.astype(np.uint8).reshape(k // 512, 16, n))


def unpack_weight(words, scales, fmt):
    g, _, n = scales.shape
    words = np.ascontiguousarray(words).reshape(g, 128, n, -1)
    if fmt == "e4m3":
        vals = words.view(ml_dtypes.float8_e4m3fn).astype(np.float64)
    else:
        nib = np.empty((g, 128, n, 4), np.uint8)
        nib[..., 0::2] = words & 0xF
        nib[..., 1::2] = words >> 4
        vals = E2M1[nib]
    vals = vals * np.repeat(np.exp2(scales.astype(np.float64) - 127.0), 8, axis=1)[..., None]
    return vals.transpose(0, 1, 3, 2).reshape(g * 512, n)


def gelu(v):
    return 0.5 * v * (1.0 + np.tanh(np.sqrt(2.0 / np.pi) * (v + 0.044715 * v**3)))


K, T, S, H, N, K2, T2, P = 1024, 4096, 1024, 512, 384, 1024, 2048, 512

def setup_inputs():
    n = np.random.standard_normal
    s = mx_kscale(K)[:, None]
    s2 = mx_kscale(K2)[:, None]
    u = mx_kscale(H)[:, None]
    tab_words, tab_scales = pack_weight(n((K, T)) * s, "e4m3")
    tab2_words, tab2_scales = pack_weight(n((K2, T2)) * s2, "e4m3")
    w2_words, w2_scales = pack_weight(1.5 * n((K, H)) / s / np.sqrt(K), "e2m1")
    return {
        "tab_words": tab_words, "tab_scales": tab_scales,
        "tab2_words": tab2_words, "tab2_scales": tab2_scales,
        "offs": striped(np.random.permutation(T)[:S]),
        "offs2": striped(np.random.permutation(T2)[:P]),
        "pos1": striped(np.random.permutation(S)[:P]),
        "w1": (n((K, H)) / s / np.sqrt(K)).astype(np.float32),
        "w2_words": w2_words, "w2_scales": w2_scales,
        "gain": (np.exp(0.4 * n(H)) * u[:, 0]).astype(np.float32),
        "w3": (n((H, N)) / u / np.sqrt(H)).astype(np.float32),
        "wv": (n((K2, N)) / s2 / np.sqrt(K2)).astype(np.float32),
    }

def reference(tab_words, tab_scales, tab2_words, tab2_scales, offs, offs2, pos1,
              w1, w2_words, w2_scales, gain, w3, wv):
    v = unpack_weight(tab_words, tab_scales, "e4m3")[:, unstriped(offs)]
    v2 = unpack_weight(tab2_words, tab2_scales, "e4m3")[:, unstriped(offs2)]
    w2 = unpack_weight(w2_words, w2_scales, "e2m1")
    a1 = mxq(f64(w1), 0, "e4m3").T @ v
    a2 = w2.T @ v
    h = f64(gain)[:, None] * (a1 + np.tanh(a1 - a2))
    y = mxq(f64(w3), 0, "e4m3").T @ mxq(h, 0, "e4m3")
    b = mxq(f64(wv), 0, "e4m3").T @ v2
    return y[:, unstriped(pos1)] * b

@@ -1,0 +1,291 @@
+from contextlib import ExitStack
+
+import concourse.mybir as mybir
+
+K, T, S, H, N, K2, T2, V = 1024, 4096, 1024, 512, 384, 1024, 2048, 512
+FLOPS = 2 * (2 * K * H * S + H * N * S + K2 * N * V)
+
+F32 = mybir.dt.float32
+BF16 = mybir.dt.bfloat16
+I32 = mybir.dt.int32
+U32 = mybir.dt.uint32
+U16 = mybir.dt.uint16
+U8 = mybir.dt.uint8
+FP8X4 = mybir.dt.float8_e4m3fn_x4
+FP4X4 = mybir.dt.float4_e2m1fn_x4
+ALU = mybir.AluOpType
+ACT = mybir.ActivationFunctionType
+
+P = 128
+CH = 128
+NCH = S // CH
+GROUPS = ((0, 2), (2, 2), (4, 2), (6, 1), (7, 1))
+GPSIMD_CHUNKS = 6
+SC_V, SC_W2, SC_V2, SC_ALL = 0, S, S + H, S + H + V
+
+
+def tile_list_pullback_view_scores_kernel(
+    tc, tab_words, tab_scales, tab2_words, tab2_scales, offs, offs2, pos1,
+    w1, w2_words, w2_scales, gain, w3, wv, out,
+):
+    nc = tc.nc
+    with ExitStack() as ctx:
+        keep = ctx.enter_context(tc.tile_pool(name="keep", bufs=1))
+        stream = ctx.enter_context(tc.tile_pool(name="stream", bufs=3))
+        work = ctx.enter_context(tc.tile_pool(name="work", bufs=3))
+        psum = ctx.enter_context(tc.psum_pool(name="psum", bufs=8))
+
+        def held(name, shape, dtype):
+            return keep.tile(shape, dtype, name=name, align_bytes=64)
+
+        def streamed(name, shape, dtype):
+            return stream.tile(shape, dtype, name=name, tag="stream", align_bytes=64)
+
+        def bank(name, shape):
+            return psum.tile(shape, F32, name=name, tag="bank")
+
+        idx = keep.tile([P, S // 16], U16, name="idx")
+        idx2 = keep.tile([P, V // 16], U16, name="idx2")
+        pick = keep.tile([P, V // 16], U16, name="pick")
+
+        ts_win = held("ts_win", [P, T], U8)
+        t2s_win = held("t2s_win", [P, T2], U8)
+        w2s_raw = held("w2s_raw", [P, H], U8)
+        planes = [held("plane%d" % a, [P, SC_ALL], U8) for a in range(2)]
+        nc.sync.dma_start(idx[:], offs)
+        nc.sync.dma_start(idx2[:], offs2)
+        for tile, rows in ((ts_win, tab_scales), (t2s_win, tab2_scales), (w2s_raw, w2_scales)):
+            nc.vector.memset(tile[0:96, :].bitcast(I32), 0)
+            nc.scalar.dma_start(
+                out=tile[96:128, :].bitcast(I32),
+                in_=rows.rearrange("a q n -> (a q) n").bitcast(I32),
+            )
+        for a in range(2):
+            nc.vector.memset(planes[a][:].bitcast(I32), 0)
+
+        def load_words(name, words, a, cols):
+            win = streamed(name, [P, cols], U32)
+            nc.sync.dma_start(
+                out=win[:].bitcast(I32),
+                in_=words[a].rearrange("p n t -> p (n t)").bitcast(I32),
+            )
+            return win
+
+        tab_win0 = load_words("tab_win0", tab_words, 0, T)
+        nc.sync.dma_start(pick[:], pos1)
+        g4 = held("g4", [P, 4], F32)
+        nc.scalar.dma_start(out=g4[:], in_=gain.rearrange("(p t) -> p t", t=4))
+        w2_raw = held("w2_raw", [P, 2, 2 * H], U8)
+        nc.sync.dma_start(
+            out=w2_raw[:].bitcast(I32), in_=w2_words.rearrange("a p n -> p a n").bitcast(I32)
+        )
+        tab_win1 = load_words("tab_win1", tab_words, 1, T)
+
+        def load_rows(name, w, a, cols, pieces):
+            raw = streamed(name, [P, 4, cols], F32)
+            rows = w[512 * a : 512 * (a + 1), :].rearrange("(p i) c -> p i c", i=4)
+            step = cols // pieces
+            for c0 in range(0, cols, step):
+                nc.sync.dma_start(out=raw[:, :, c0 : c0 + step], in_=rows[:, :, c0 : c0 + step])
+            return raw
+
+        w1_raw0 = load_rows("w1_raw0", w1, 0, H, 1)
+
+        vs_g = held("vs_g", [P, S], U8)
+        v2s_g = held("v2s_g", [P, V], U8)
+        staged = held("staged", [P, SC_ALL], U8)
+        nc.vector.tensor_copy(vs_g[:], ts_win[:].indirect(idx[:]))
+        nc.vector.tensor_copy(v2s_g[:], t2s_win[:].indirect(idx2[:]))
+        nc.vector.tensor_copy(
+            staged[:, SC_W2:SC_V2].rearrange("p (t m) -> p t m", t=4),
+            w2s_raw[:].rearrange("p (m t) -> p t m", t=4),
+        )
+        nc.vector.tensor_copy(staged[96:128, SC_V:SC_W2].bitcast(I32), vs_g[96:128, :].bitcast(I32))
+        nc.vector.tensor_copy(staged[96:128, SC_V2:SC_ALL].bitcast(I32), v2s_g[96:128, :].bitcast(I32))
+        for a, queue in ((0, nc.scalar), (1, nc.gpsimd)):
+            for q in range(4):
+                row = 96 + 16 * a + 4 * q
+                queue.dma_start(
+                    out=planes[a][32 * q : 32 * q + 4, :].bitcast(I32),
+                    in_=staged[row : row + 4, :].bitcast(I32),
+                )
+
+        gains = held("gains", [P, CH, 4], F32)
+        nc.scalar.activation(gains[:], g4[:].unsqueeze(1).to_broadcast([P, CH, 4]), ACT.Copy)
+
+        v_words = [held("v_words%d" % a, [P, S], U32) for a in range(2)]
+        nc.vector.tensor_copy(v_words[0][:], tab_win0[:].indirect(idx[:]))
+        w2_perm = [held("w2_perm%d" % a, [P, 2 * H], U8) for a in range(2)]
+        for a in range(2):
+            nc.vector.tensor_copy(
+                w2_perm[a][:].rearrange("p (t m b) -> p t m b", t=4, b=2),
+                w2_raw[:, a, :].rearrange("p (m t b) -> p t m b", t=4, b=2),
+            )
+
+        def first_stage_pass(acc, c, a, lhs, lhs_scale):
+            cols = slice(c * CH, (c + 1) * CH)
+            for t in range(4):
+                nc.tensor.matmul_mx(
+                    out=acc[:, t, :],
+                    lhsT=lhs(t),
+                    lhsT_scale=lhs_scale(t),
+                    rhs=v_words[a][:, cols].bitcast(FP8X4),
+                    rhs_scale=planes[a][:, cols],
+                    start=(a == 0 and t == 0),
+                    stop=(a == 1 and t == 3),
+                )
+
+        def a2_pass(acc, c, a):
+            first_stage_pass(
+                acc, c, a,
+                lambda t: w2_perm[a][:, 256 * t : 256 * (t + 1)].bitcast(FP4X4),
+                lambda t: planes[a][:, SC_W2 + 128 * t : SC_W2 + 128 * (t + 1)],
+            )
+
+        a2_acc = [bank("a2_%d" % c, [P, 4, CH]) for c in range(NCH)]
+        for c in range(NCH):
+            a2_pass(a2_acc[c], c, 0)
+        a2_sb = [held("a2_sb%d" % c, [P, CH, 4], F32) for c in range(NCH)]
+        for half in range(2):
+            nc.vector.tensor_copy(
+                v_words[1][:, 512 * half : 512 * (half + 1)],
+                tab_win1[:].indirect(idx[:, 32 * half : 32 * (half + 1)]),
+            )
+            for c in range(4 * half, 4 * half + 4):
+                a2_pass(a2_acc[c], c, 1)
+                nc.scalar.copy(a2_sb[c][:], a2_acc[c][:].rearrange("p t j -> p j t"))
+
+        w1_raw1 = load_rows("w1_raw1", w1, 1, H, 2)
+        w1_bf = [held("w1_bf%d" % a, [P, 4, P, 4], BF16) for a in range(2)]
+        w1_q = [held("w1_q%d" % a, [P, H], U32) for a in range(2)]
+        w1_s = [held("w1_s%d" % a, [P, H], U8) for a in range(2)]
+
+        def round_w1(copy, a, raw, m0, m1):
+            copy(
+                w1_bf[a][:, :, m0:m1, :].rearrange("p t m i -> p m i t"),
+                raw[:, :, 4 * m0 : 4 * m1].rearrange("p i (m t) -> p m i t", t=4),
+            )
+
+        def quantise(codes, scales, values):
+            nc.vector.quantize_mx(out=codes.bitcast(FP8X4), scales=scales, in_=values)
+
+        round_w1(nc.vector.tensor_copy, 0, w1_raw0, 0, 128)
+        quantise(w1_q[0][:], w1_s[0][:], w1_bf[0][:].rearrange("p t m i -> p (t m i)"))
+        round_w1(nc.vector.tensor_copy, 1, w1_raw1, 0, 64)
+        round_w1(nc.vector.tensor_copy, 1, w1_raw1, 64, 128)
+        for u in range(2):
+            quantise(
+                w1_q[1][:, 256 * u : 256 * (u + 1)],
+                w1_s[1][:, 256 * u : 256 * (u + 1)],
+                w1_bf[1][:, 2 * u : 2 * u + 2].rearrange("p t m i -> p (t m i)"),
+            )
+
+        def a1_pass(acc, c, a):
+            first_stage_pass(
+                acc, c, a,
+                lambda t: w1_q[a][:, 128 * t : 128 * (t + 1)].bitcast(FP8X4),
+                lambda t: w1_s[a][:, 128 * t : 128 * (t + 1)],
+            )
+
+        def plain_weight(name, w, a, copy, pieces):
+            raw = load_rows(name + "_raw", w, a, N, 1)
+            rounded = held(name + "_bf", [P, N, 4], BF16)
+            codes = held(name + "_q", [P, N], U32)
+            scales = held(name + "_s", [P, N], U8)
+            step = N // pieces
+            for c0 in range(0, N, step):
+                copy(
+                    rounded[:, c0 : c0 + step, :].rearrange("p (c s) i -> p c i s", s=4),
+                    raw[:, :, c0 : c0 + step].rearrange("p i (c s) -> p c i s", s=4),
+                )
+            quantise(codes[:], scales[:], rounded[:].rearrange("p c i -> p (c i)"))
+            return codes, scales
+
+        h_q = held("h_q", [P, S], U32)
+        h_s = held("h_s", [P, S], U8)
+        y_sb = [held("y_sb%d" % n, [P, S], F32) for n in range(3)]
+        b_sb = [held("b_sb%d" % n, [P, V], F32) for n in range(3)]
+        v2_words = [held("v2_words%d" % a, [P, V], U32) for a in range(2)]
+        h_bf = held("h_bf", [P, S, 4], BF16)
+        state = {}
+
+        def front(c):
+            acc = bank("a1_%d" % c, [P, 4, CH])
+            a1_pass(acc, c, 0)
+            a1_pass(acc, c, 1)
+            a1 = acc[:].rearrange("p t j -> p j t")
+            diff = work.tile([P, CH, 4], F32, name="diff")
+            nc.vector.tensor_tensor(diff[:], a1, a2_sb[c][:], ALU.subtract)
+            th = work.tile([P, CH, 4], F32, name="th")
+            nc.scalar.activation(th[:], diff[:], ACT.Tanh)
+            state[c] = (a1, th)
+
+        def back(c):
+            a1, th = state[c]
+            total = work.tile([P, CH, 4], F32, name="total")
+            nc.vector.tensor_tensor(total[:], a1, th[:], ALU.add)
+            engine = nc.gpsimd if c < GPSIMD_CHUNKS else nc.vector
+            engine.tensor_tensor(h_bf[:, c * CH : (c + 1) * CH, :], total[:], gains[:], ALU.mult)
+
+        def second_stage(c0, count):
+            cols = slice(c0 * CH, (c0 + count) * CH)
+            quantise(h_q[:, cols], h_s[:, cols], h_bf[:, cols, :].rearrange("p j t -> p (j t)"))
+            w3_q, w3_s = state["w3"]
+            for n in range(3):
+                acc = bank("y_%d_%d" % (c0, n), [P, count * CH])
+                nc.tensor.matmul_mx(
+                    out=acc[:],
+                    lhsT=w3_q[:, 128 * n : 128 * (n + 1)].bitcast(FP8X4),
+                    lhsT_scale=w3_s[:, 128 * n : 128 * (n + 1)],
+                    rhs=h_q[:, cols].bitcast(FP8X4),
+                    rhs_scale=h_s[:, cols],
+                    start=True,
+                    stop=True,
+                )
+                nc.scalar.copy(y_sb[n][:, cols], acc[:])
+
+        def view_operands(a):
+            if a == 0:
+                state["wv0"] = plain_weight("wv0", wv, 0, nc.scalar.copy, 3)
+            else:
+                state["wv1"] = plain_weight("wv1", wv, 1, nc.vector.tensor_copy, 1)
+            win = load_words("tab2_win%d" % a, tab2_words, a, T2)
+            nc.vector.tensor_copy(v2_words[a][:], win[:].indirect(idx2[:]))
+
+        def view_scores():
+            for n in range(3):
+                acc = bank("b_%d" % n, [P, V])
+                for a in range(2):
+                    codes, scales = state["wv%d" % a]
+                    nc.tensor.matmul_mx(
+                        out=acc[:],
+                        lhsT=codes[:, 128 * n : 128 * (n + 1)].bitcast(FP8X4),
+                        lhsT_scale=scales[:, 128 * n : 128 * (n + 1)],
+                        rhs=v2_words[a][:].bitcast(FP8X4),
+                        rhs_scale=planes[a][:, SC_V2:SC_ALL],
+                        start=(a == 0),
+                        stop=(a == 1),
+                    )
+                nc.scalar.copy(b_sb[n][:], acc[:])
+
+        ends = {c0 + count - 1: (c0, count) for c0, count in GROUPS}
+        for step in range(NCH + 2):
+            if step < NCH:
+                front(step)
+            if 1 <= step <= NCH:
+                back(step - 1)
+            if step == 1:
+                state["w3"] = plain_weight("w3", w3, 0, nc.scalar.copy, 3)
+            if step == 3:
+                view_operands(0)
+            if step == 5:
+                view_operands(1)
+            if step == 6:
+                view_scores()
+            if step - 2 in ends:
+                second_stage(*ends[step - 2])
+
+        for n in range(3):
+            res = held("res%d" % n, [P, V], F32)
+            nc.vector.tensor_tensor(res[:], y_sb[n][:].indirect(pick[:]), b_sb[n][:], ALU.mult)
+            nc.sync.dma_start(out=out[128 * n : 128 * (n + 1), :], in_=res[:])

@@ -20,7 +20,7 @@ P = 128
 CH = 128
 NCH = S // CH
 GROUPS = ((0, 2), (2, 2), (4, 2), (6, 1), (7, 1))
-GPSIMD_CHUNKS = 6
+GPSIMD_CHUNKS = 0
 SC_V, SC_W2, SC_V2, SC_ALL = 0, S, S + H, S + H + V
 
 
@@ -33,7 +33,7 @@ def tile_list_pullback_view_scores_kernel(
         keep = ctx.enter_context(tc.tile_pool(name="keep", bufs=1))
         stream = ctx.enter_context(tc.tile_pool(name="stream", bufs=3))
         work = ctx.enter_context(tc.tile_pool(name="work", bufs=3))
-        psum = ctx.enter_context(tc.psum_pool(name="psum", bufs=8))
+        psum = ctx.enter_context(tc.psum_pool(name="psum", bufs=1))
 
         def held(name, shape, dtype):
             return keep.tile(shape, dtype, name=name, align_bytes=64)
@@ -41,8 +41,10 @@ def tile_list_pullback_view_scores_kernel(
         def streamed(name, shape, dtype):
             return stream.tile(shape, dtype, name=name, tag="stream", align_bytes=64)
 
-        def bank(name, shape):
-            return psum.tile(shape, F32, name=name, tag="bank")
+        def bank(name, shape, near=False):
+            if near:
+                return psum.tile(shape, F32, name=name, tag="near", bufs=3)
+            return psum.tile(shape, F32, name=name, tag="far", bufs=5)
 
         idx = keep.tile([P, S // 16], U16, name="idx")
         idx2 = keep.tile([P, V // 16], U16, name="idx2")
@@ -52,16 +54,21 @@ def tile_list_pullback_view_scores_kernel(
         t2s_win = held("t2s_win", [P, T2], U8)
         w2s_raw = held("w2s_raw", [P, H], U8)
         planes = [held("plane%d" % a, [P, SC_ALL], U8) for a in range(2)]
-        nc.sync.dma_start(idx[:], offs)
-        nc.sync.dma_start(idx2[:], offs2)
-        for tile, rows in ((ts_win, tab_scales), (t2s_win, tab2_scales), (w2s_raw, w2_scales)):
-            nc.vector.memset(tile[0:96, :].bitcast(I32), 0)
-            nc.scalar.dma_start(
+
+        def load_scale_rows(tile, rows):
+            nc.gpsimd.memset(tile[0:96, :].bitcast(I32), 0)
+            nc.sync.dma_start(
                 out=tile[96:128, :].bitcast(I32),
                 in_=rows.rearrange("a q n -> (a q) n").bitcast(I32),
             )
+
+        nc.sync.dma_start(idx[:], offs)
+        load_scale_rows(ts_win, tab_scales)
+        nc.sync.dma_start(idx2[:], offs2)
+        load_scale_rows(t2s_win, tab2_scales)
+        load_scale_rows(w2s_raw, w2_scales)
         for a in range(2):
-            nc.vector.memset(planes[a][:].bitcast(I32), 0)
+            nc.gpsimd.memset(planes[a][:].bitcast(I32), 0)
 
         def load_words(name, words, a, cols):
             win = streamed(name, [P, cols], U32)
@@ -71,15 +78,16 @@ def tile_list_pullback_view_scores_kernel(
             )
             return win
 
-        tab_win0 = load_words("tab_win0", tab_words, 0, T)
-        nc.sync.dma_start(pick[:], pos1)
         g4 = held("g4", [P, 4], F32)
-        nc.scalar.dma_start(out=g4[:], in_=gain.rearrange("(p t) -> p t", t=4))
-        w2_raw = held("w2_raw", [P, 2, 2 * H], U8)
+        nc.sync.dma_start(out=g4[:], in_=gain.rearrange("(p t) -> p t", t=4))
+
+        w2_raw = streamed("w2_raw", [P, 2, 2 * H], U8)
         nc.sync.dma_start(
             out=w2_raw[:].bitcast(I32), in_=w2_words.rearrange("a p n -> p a n").bitcast(I32)
         )
+        tab_win0 = load_words("tab_win0", tab_words, 0, T)
         tab_win1 = load_words("tab_win1", tab_words, 1, T)
+        nc.sync.dma_start(pick[:], pos1)
 
         def load_rows(name, w, a, cols, pieces):
             raw = streamed(name, [P, 4, cols], F32)
@@ -89,8 +97,16 @@ def tile_list_pullback_view_scores_kernel(
                 nc.sync.dma_start(out=raw[:, :, c0 : c0 + step], in_=rows[:, :, c0 : c0 + step])
             return raw
 
-        w1_raw0 = load_rows("w1_raw0", w1, 0, H, 1)
+        w1_bf = [held("w1_bf%d" % a, [P, 4, P, 4], BF16) for a in range(2)]
 
+        def round_w1(a, raw, m0, m1):
+            nc.vector.tensor_copy(
+                w1_bf[a][:, :, m0:m1, :].rearrange("p t m i -> p m i t"),
+                raw[:, :, 4 * m0 : 4 * m1].rearrange("p i (m t) -> p m i t", t=4),
+            )
+
+        gains = held("gains", [P, CH, 4], F32)
+        nc.scalar.activation(gains[:], g4[:].unsqueeze(1).to_broadcast([P, CH, 4]), ACT.Copy)
         vs_g = held("vs_g", [P, S], U8)
         v2s_g = held("v2s_g", [P, V], U8)
         staged = held("staged", [P, SC_ALL], U8)
@@ -102,7 +118,7 @@ def tile_list_pullback_view_scores_kernel(
         )
         nc.vector.tensor_copy(staged[96:128, SC_V:SC_W2].bitcast(I32), vs_g[96:128, :].bitcast(I32))
         nc.vector.tensor_copy(staged[96:128, SC_V2:SC_ALL].bitcast(I32), v2s_g[96:128, :].bitcast(I32))
-        for a, queue in ((0, nc.scalar), (1, nc.gpsimd)):
+        for a, queue in ((0, nc.scalar), (1, nc.scalar)):
             for q in range(4):
                 row = 96 + 16 * a + 4 * q
                 queue.dma_start(
@@ -110,17 +126,23 @@ def tile_list_pullback_view_scores_kernel(
                     in_=staged[row : row + 4, :].bitcast(I32),
                 )
 
-        gains = held("gains", [P, CH, 4], F32)
-        nc.scalar.activation(gains[:], g4[:].unsqueeze(1).to_broadcast([P, CH, 4]), ACT.Copy)
 
         v_words = [held("v_words%d" % a, [P, S], U32) for a in range(2)]
-        nc.vector.tensor_copy(v_words[0][:], tab_win0[:].indirect(idx[:]))
         w2_perm = [held("w2_perm%d" % a, [P, 2 * H], U8) for a in range(2)]
         for a in range(2):
             nc.vector.tensor_copy(
                 w2_perm[a][:].rearrange("p (t m b) -> p t m b", t=4, b=2),
                 w2_raw[:, a, :].rearrange("p (m t b) -> p t m b", t=4, b=2),
             )
+
+        nc.vector.tensor_copy(v_words[0][:], tab_win0[:].indirect(idx[:]))
+        w1_raw = [load_rows("w1_raw0", w1, 0, H, 1), load_rows("w1_raw1", w1, 1, H, 2)]
+        w1_q = [held("w1_q%d" % a, [P, H], U32) for a in range(2)]
+        w1_s = [held("w1_s%d" % a, [P, H], U8) for a in range(2)]
+
+        def quantise(codes, scales, values):
+            nc.vector.quantize_mx(out=codes.bitcast(FP8X4), scales=scales, in_=values)
+
 
         def first_stage_pass(acc, c, a, lhs, lhs_scale):
             cols = slice(c * CH, (c + 1) * CH)
@@ -142,7 +164,7 @@ def tile_list_pullback_view_scores_kernel(
                 lambda t: planes[a][:, SC_W2 + 128 * t : SC_W2 + 128 * (t + 1)],
             )
 
-        a2_acc = [bank("a2_%d" % c, [P, 4, CH]) for c in range(NCH)]
+        a2_acc = [bank("a2_%d" % c, [P, 4, CH], near=c < 3) for c in range(NCH)]
         for c in range(NCH):
             a2_pass(a2_acc[c], c, 0)
         a2_sb = [held("a2_sb%d" % c, [P, CH, 4], F32) for c in range(NCH)]
@@ -155,24 +177,10 @@ def tile_list_pullback_view_scores_kernel(
                 a2_pass(a2_acc[c], c, 1)
                 nc.scalar.copy(a2_sb[c][:], a2_acc[c][:].rearrange("p t j -> p j t"))
 
-        w1_raw1 = load_rows("w1_raw1", w1, 1, H, 2)
-        w1_bf = [held("w1_bf%d" % a, [P, 4, P, 4], BF16) for a in range(2)]
-        w1_q = [held("w1_q%d" % a, [P, H], U32) for a in range(2)]
-        w1_s = [held("w1_s%d" % a, [P, H], U8) for a in range(2)]
-
-        def round_w1(copy, a, raw, m0, m1):
-            copy(
-                w1_bf[a][:, :, m0:m1, :].rearrange("p t m i -> p m i t"),
-                raw[:, :, 4 * m0 : 4 * m1].rearrange("p i (m t) -> p m i t", t=4),
-            )
-
-        def quantise(codes, scales, values):
-            nc.vector.quantize_mx(out=codes.bitcast(FP8X4), scales=scales, in_=values)
-
-        round_w1(nc.vector.tensor_copy, 0, w1_raw0, 0, 128)
+        round_w1(0, w1_raw[0], 0, 128)
         quantise(w1_q[0][:], w1_s[0][:], w1_bf[0][:].rearrange("p t m i -> p (t m i)"))
-        round_w1(nc.vector.tensor_copy, 1, w1_raw1, 0, 64)
-        round_w1(nc.vector.tensor_copy, 1, w1_raw1, 64, 128)
+        round_w1(1, w1_raw[1], 0, 64)
+        round_w1(1, w1_raw[1], 64, 128)
         for u in range(2):
             quantise(
                 w1_q[1][:, 256 * u : 256 * (u + 1)],
@@ -210,7 +218,7 @@ def tile_list_pullback_view_scores_kernel(
         state = {}
 
         def front(c):
-            acc = bank("a1_%d" % c, [P, 4, CH])
+            acc = bank("a1_%d" % c, [P, 4, CH], near=True)
             a1_pass(acc, c, 0)
             a1_pass(acc, c, 1)
             a1 = acc[:].rearrange("p t j -> p j t")
@@ -248,7 +256,7 @@ def tile_list_pullback_view_scores_kernel(
             if a == 0:
                 state["wv0"] = plain_weight("wv0", wv, 0, nc.scalar.copy, 3)
             else:
-                state["wv1"] = plain_weight("wv1", wv, 1, nc.vector.tensor_copy, 1)
+                state["wv1"] = plain_weight("wv1", wv, 1, nc.scalar.copy, 3)
             win = load_words("tab2_win%d" % a, tab2_words, a, T2)
             nc.vector.tensor_copy(v2_words[a][:], win[:].indirect(idx2[:]))
 

@@ -1,6 +1,7 @@
 from contextlib import ExitStack
 
 import concourse.mybir as mybir
+from concourse.masks import make_identity
 
 K, T, S, H, N, K2, T2, V = 1024, 4096, 1024, 512, 384, 1024, 2048, 512
 FLOPS = 2 * (2 * K * H * S + H * N * S + K2 * N * V)
@@ -20,7 +21,6 @@ P = 128
 CH = 128
 NCH = S // CH
 GROUPS = ((0, 2), (2, 2), (4, 2), (6, 1), (7, 1))
-GPSIMD_CHUNKS = 0
 SC_V, SC_W2, SC_V2, SC_ALL = 0, S, S + H, S + H + V
 
 
@@ -41,34 +41,20 @@ def tile_list_pullback_view_scores_kernel(
         def streamed(name, shape, dtype):
             return stream.tile(shape, dtype, name=name, tag="stream", align_bytes=64)
 
-        def bank(name, shape, near=False):
-            if near:
-                return psum.tile(shape, F32, name=name, tag="near", bufs=3)
+        def near_bank(name, shape):
+            return psum.tile(shape, F32, name=name, tag="near", bufs=3)
+
+        def far_bank(name, shape):
             return psum.tile(shape, F32, name=name, tag="far", bufs=5)
 
-        idx = keep.tile([P, S // 16], U16, name="idx")
-        idx2 = keep.tile([P, V // 16], U16, name="idx2")
-        pick = keep.tile([P, V // 16], U16, name="pick")
-
-        ts_win = held("ts_win", [P, T], U8)
-        t2s_win = held("t2s_win", [P, T2], U8)
-        w2s_raw = held("w2s_raw", [P, H], U8)
-        planes = [held("plane%d" % a, [P, SC_ALL], U8) for a in range(2)]
+        def quantise(codes, scales, values):
+            nc.vector.quantize_mx(out=codes.bitcast(FP8X4), scales=scales, in_=values)
 
         def load_scale_rows(tile, rows):
-            nc.gpsimd.memset(tile[0:96, :].bitcast(I32), 0)
             nc.sync.dma_start(
                 out=tile[96:128, :].bitcast(I32),
                 in_=rows.rearrange("a q n -> (a q) n").bitcast(I32),
             )
-
-        nc.sync.dma_start(idx[:], offs)
-        load_scale_rows(ts_win, tab_scales)
-        nc.sync.dma_start(idx2[:], offs2)
-        load_scale_rows(t2s_win, tab2_scales)
-        load_scale_rows(w2s_raw, w2_scales)
-        for a in range(2):
-            nc.gpsimd.memset(planes[a][:].bitcast(I32), 0)
 
         def load_words(name, words, a, cols):
             win = streamed(name, [P, cols], U32)
@@ -78,17 +64,6 @@ def tile_list_pullback_view_scores_kernel(
             )
             return win
 
-        g4 = held("g4", [P, 4], F32)
-        nc.sync.dma_start(out=g4[:], in_=gain.rearrange("(p t) -> p t", t=4))
-
-        w2_raw = streamed("w2_raw", [P, 2, 2 * H], U8)
-        nc.sync.dma_start(
-            out=w2_raw[:].bitcast(I32), in_=w2_words.rearrange("a p n -> p a n").bitcast(I32)
-        )
-        tab_win0 = load_words("tab_win0", tab_words, 0, T)
-        tab_win1 = load_words("tab_win1", tab_words, 1, T)
-        nc.sync.dma_start(pick[:], pos1)
-
         def load_rows(name, w, a, cols, pieces):
             raw = streamed(name, [P, 4, cols], F32)
             rows = w[512 * a : 512 * (a + 1), :].rearrange("(p i) c -> p i c", i=4)
@@ -97,90 +72,118 @@ def tile_list_pullback_view_scores_kernel(
                 nc.sync.dma_start(out=raw[:, :, c0 : c0 + step], in_=rows[:, :, c0 : c0 + step])
             return raw
 
-        w1_bf = [held("w1_bf%d" % a, [P, 4, P, 4], BF16) for a in range(2)]
+        idx = keep.tile([P, S // 16], U16, name="idx")
+        idx2 = keep.tile([P, V // 16], U16, name="idx2")
+        pick = keep.tile([P, V // 16], U16, name="pick")
+        ts_win = held("ts_win", [P, T], U8)
+        t2s_win = held("t2s_win", [P, T2], U8)
+        w2s_raw = held("w2s_raw", [P, H], U8)
+        gain_rows = held("gain_rows", [P, P], F32)
+        planes = [held("plane%d" % a, [P, SC_ALL], U8) for a in range(2)]
+        nc.vector.memset(ts_win[0:96, :].bitcast(I32), 0)
+        nc.vector.memset(t2s_win[0:96, :].bitcast(I32), 0)
+        nc.vector.memset(gain_rows[0:96, :], 0.0)
+        nc.vector.memset(gain_rows[96:124, :], 0.0)
+        for a in range(2):
+            nc.vector.memset(planes[a][:].bitcast(I32), 0)
 
-        def round_w1(a, raw, m0, m1):
-            nc.vector.tensor_copy(
-                w1_bf[a][:, :, m0:m1, :].rearrange("p t m i -> p m i t"),
-                raw[:, :, 4 * m0 : 4 * m1].rearrange("p i (m t) -> p m i t", t=4),
-            )
+        nc.sync.dma_start(idx[:], offs)
+        load_scale_rows(ts_win, tab_scales)
+        nc.sync.dma_start(idx2[:], offs2)
+        load_scale_rows(t2s_win, tab2_scales)
+        load_scale_rows(w2s_raw, w2_scales)
+        nc.sync.dma_start(
+            out=gain_rows[124:128, :], in_=gain.rearrange("(m t s) -> t m s", t=4, s=4)
+        )
+        w2_raw = streamed("w2_raw", [P, 2, 2 * H], U8)
+        nc.sync.dma_start(
+            out=w2_raw[:].bitcast(I32), in_=w2_words.rearrange("a p n -> p a n").bitcast(I32)
+        )
+        tab_win = [load_words("tab_win%d" % a, tab_words, a, T) for a in range(2)]
+        nc.sync.dma_start(pick[:], pos1)
 
+        ident = held("ident", [P, P], F32)
+        make_identity(nc, ident[:])
+        gain_cols = far_bank("gain_cols", [P, P])
+        nc.tensor.transpose(gain_cols[:], gain_rows[:], ident[:])
         gains = held("gains", [P, CH, 4], F32)
-        nc.scalar.activation(gains[:], g4[:].unsqueeze(1).to_broadcast([P, CH, 4]), ACT.Copy)
+        nc.scalar.activation(
+            gains[:], gain_cols[:, 124:128].unsqueeze(1).to_broadcast([P, CH, 4]), ACT.Copy
+        )
+
         vs_g = held("vs_g", [P, S], U8)
         v2s_g = held("v2s_g", [P, V], U8)
         staged = held("staged", [P, SC_ALL], U8)
         nc.vector.tensor_copy(vs_g[:], ts_win[:].indirect(idx[:]))
         nc.vector.tensor_copy(v2s_g[:], t2s_win[:].indirect(idx2[:]))
-        nc.vector.tensor_copy(
-            staged[:, SC_W2:SC_V2].rearrange("p (t m) -> p t m", t=4),
-            w2s_raw[:].rearrange("p (m t) -> p t m", t=4),
-        )
         nc.vector.tensor_copy(staged[96:128, SC_V:SC_W2].bitcast(I32), vs_g[96:128, :].bitcast(I32))
+        nc.vector.tensor_copy(
+            staged[96:128, SC_W2:SC_V2].bitcast(I32).rearrange("p (t m) -> p t m", t=4),
+            w2s_raw[96:128, :].bitcast(I32).rearrange("p (m t) -> p t m", t=4),
+        )
         nc.vector.tensor_copy(staged[96:128, SC_V2:SC_ALL].bitcast(I32), v2s_g[96:128, :].bitcast(I32))
-        for a, queue in ((0, nc.scalar), (1, nc.scalar)):
+        for a in range(2):
             for q in range(4):
                 row = 96 + 16 * a + 4 * q
-                queue.dma_start(
+                nc.scalar.dma_start(
                     out=planes[a][32 * q : 32 * q + 4, :].bitcast(I32),
                     in_=staged[row : row + 4, :].bitcast(I32),
                 )
 
+        w2_perm = held("w2_perm", [P, 2, 2 * H], U8)
+        nc.vector.tensor_copy(
+            w2_perm[:].bitcast(I32).rearrange("p a (t m w) -> p a t m w", t=4, w=2),
+            w2_raw[:].bitcast(I32).rearrange("p a (m t w) -> p a t m w", t=4, w=2),
+        )
+        w1_raw = [load_rows("w1_raw0", w1, 0, H, 1), load_rows("w1_raw1", w1, 1, H, 2)]
 
         v_words = [held("v_words%d" % a, [P, S], U32) for a in range(2)]
-        w2_perm = [held("w2_perm%d" % a, [P, 2 * H], U8) for a in range(2)]
-        for a in range(2):
-            nc.vector.tensor_copy(
-                w2_perm[a][:].rearrange("p (t m b) -> p t m b", t=4, b=2),
-                w2_raw[:, a, :].rearrange("p (m t b) -> p t m b", t=4, b=2),
+        a2_sb = held("a2_sb", [P, 4, S], F32)
+        a2_acc = {}
+        for half in range(2):
+            for t in range(4):
+                place = near_bank if 4 * half + t < 3 else far_bank
+                a2_acc[half, t] = place("a2_%d_%d" % (half, t), [P, 512])
+
+        def a2_pass(half, t, a):
+            cols = slice(512 * half, 512 * (half + 1))
+            nc.tensor.matmul_mx(
+                out=a2_acc[half, t][:],
+                lhsT=w2_perm[:, a, 256 * t : 256 * (t + 1)].bitcast(FP4X4),
+                lhsT_scale=planes[a][:, SC_W2 + 128 * t : SC_W2 + 128 * (t + 1)],
+                rhs=v_words[a][:, cols].bitcast(FP8X4),
+                rhs_scale=planes[a][:, cols],
+                start=(a == 0),
+                stop=(a == 1),
             )
 
-        nc.vector.tensor_copy(v_words[0][:], tab_win0[:].indirect(idx[:]))
-        w1_raw = [load_rows("w1_raw0", w1, 0, H, 1), load_rows("w1_raw1", w1, 1, H, 2)]
+        nc.vector.tensor_copy(v_words[0][:], tab_win[0][:].indirect(idx[:]))
+        for half in range(2):
+            for t in range(4):
+                a2_pass(half, t, 0)
+        for half in range(2):
+            cols = slice(512 * half, 512 * (half + 1))
+            nc.vector.tensor_copy(
+                v_words[1][:, cols], tab_win[1][:].indirect(idx[:, 32 * half : 32 * (half + 1)])
+            )
+            for t in range(4):
+                a2_pass(half, t, 1)
+                nc.scalar.copy(a2_sb[:, t, cols], a2_acc[half, t][:])
+
+        w1_bf = [held("w1_bf%d" % a, [P, 4, P, 4], BF16) for a in range(2)]
         w1_q = [held("w1_q%d" % a, [P, H], U32) for a in range(2)]
         w1_s = [held("w1_s%d" % a, [P, H], U8) for a in range(2)]
 
-        def quantise(codes, scales, values):
-            nc.vector.quantize_mx(out=codes.bitcast(FP8X4), scales=scales, in_=values)
-
-
-        def first_stage_pass(acc, c, a, lhs, lhs_scale):
-            cols = slice(c * CH, (c + 1) * CH)
-            for t in range(4):
-                nc.tensor.matmul_mx(
-                    out=acc[:, t, :],
-                    lhsT=lhs(t),
-                    lhsT_scale=lhs_scale(t),
-                    rhs=v_words[a][:, cols].bitcast(FP8X4),
-                    rhs_scale=planes[a][:, cols],
-                    start=(a == 0 and t == 0),
-                    stop=(a == 1 and t == 3),
-                )
-
-        def a2_pass(acc, c, a):
-            first_stage_pass(
-                acc, c, a,
-                lambda t: w2_perm[a][:, 256 * t : 256 * (t + 1)].bitcast(FP4X4),
-                lambda t: planes[a][:, SC_W2 + 128 * t : SC_W2 + 128 * (t + 1)],
-            )
-
-        a2_acc = [bank("a2_%d" % c, [P, 4, CH], near=c < 3) for c in range(NCH)]
-        for c in range(NCH):
-            a2_pass(a2_acc[c], c, 0)
-        a2_sb = [held("a2_sb%d" % c, [P, CH, 4], F32) for c in range(NCH)]
-        for half in range(2):
+        def round_w1(a, c0, c1):
             nc.vector.tensor_copy(
-                v_words[1][:, 512 * half : 512 * (half + 1)],
-                tab_win1[:].indirect(idx[:, 32 * half : 32 * (half + 1)]),
+                w1_bf[a][:, :, c0 // 4 : c1 // 4, :].rearrange("p t (m s) i -> p t m i s", s=4),
+                w1_raw[a][:, :, c0:c1].rearrange("p i (m t s) -> p t m i s", t=4, s=4),
             )
-            for c in range(4 * half, 4 * half + 4):
-                a2_pass(a2_acc[c], c, 1)
-                nc.scalar.copy(a2_sb[c][:], a2_acc[c][:].rearrange("p t j -> p j t"))
 
-        round_w1(0, w1_raw[0], 0, 128)
+        round_w1(0, 0, H)
         quantise(w1_q[0][:], w1_s[0][:], w1_bf[0][:].rearrange("p t m i -> p (t m i)"))
-        round_w1(1, w1_raw[1], 0, 64)
-        round_w1(1, w1_raw[1], 64, 128)
+        round_w1(1, 0, H // 2)
+        round_w1(1, H // 2, H)
         for u in range(2):
             quantise(
                 w1_q[1][:, 256 * u : 256 * (u + 1)],
@@ -188,59 +191,63 @@ def tile_list_pullback_view_scores_kernel(
                 w1_bf[1][:, 2 * u : 2 * u + 2].rearrange("p t m i -> p (t m i)"),
             )
 
-        def a1_pass(acc, c, a):
-            first_stage_pass(
-                acc, c, a,
-                lambda t: w1_q[a][:, 128 * t : 128 * (t + 1)].bitcast(FP8X4),
-                lambda t: w1_s[a][:, 128 * t : 128 * (t + 1)],
-            )
-
-        def plain_weight(name, w, a, copy, pieces):
-            raw = load_rows(name + "_raw", w, a, N, 1)
+        def round_and_quantise(name, raw):
             rounded = held(name + "_bf", [P, N, 4], BF16)
             codes = held(name + "_q", [P, N], U32)
             scales = held(name + "_s", [P, N], U8)
-            step = N // pieces
-            for c0 in range(0, N, step):
-                copy(
-                    rounded[:, c0 : c0 + step, :].rearrange("p (c s) i -> p c i s", s=4),
-                    raw[:, :, c0 : c0 + step].rearrange("p i (c s) -> p c i s", s=4),
+            for c0 in range(0, N, P):
+                nc.scalar.copy(
+                    rounded[:, c0 : c0 + P, :].rearrange("p (c s) i -> p c i s", s=4),
+                    raw[:, :, c0 : c0 + P].rearrange("p i (c s) -> p c i s", s=4),
                 )
             quantise(codes[:], scales[:], rounded[:].rearrange("p c i -> p (c i)"))
             return codes, scales
 
+        h_bf = held("h_bf", [P, S, 4], BF16)
         h_q = held("h_q", [P, S], U32)
         h_s = held("h_s", [P, S], U8)
         y_sb = [held("y_sb%d" % n, [P, S], F32) for n in range(3)]
         b_sb = [held("b_sb%d" % n, [P, V], F32) for n in range(3)]
         v2_words = [held("v2_words%d" % a, [P, V], U32) for a in range(2)]
-        h_bf = held("h_bf", [P, S, 4], BF16)
         state = {}
 
-        def front(c):
-            acc = bank("a1_%d" % c, [P, 4, CH], near=True)
-            a1_pass(acc, c, 0)
-            a1_pass(acc, c, 1)
-            a1 = acc[:].rearrange("p t j -> p j t")
-            diff = work.tile([P, CH, 4], F32, name="diff")
-            nc.vector.tensor_tensor(diff[:], a1, a2_sb[c][:], ALU.subtract)
+        def difference(c):
+            cols = slice(c * CH, (c + 1) * CH)
+            acc = near_bank("a1_%d" % c, [P, 4, CH])
+            for a in range(2):
+                for t in range(4):
+                    nc.tensor.matmul_mx(
+                        out=acc[:, t, :],
+                        lhsT=w1_q[a][:, 128 * t : 128 * (t + 1)].bitcast(FP8X4),
+                        lhsT_scale=w1_s[a][:, 128 * t : 128 * (t + 1)],
+                        rhs=v_words[a][:, cols].bitcast(FP8X4),
+                        rhs_scale=planes[a][:, cols],
+                        start=(a == 0 and t == 0),
+                        stop=(a == 1 and t == 3),
+                    )
+            diff = work.tile([P, 4, CH], F32, name="diff")
+            nc.vector.tensor_tensor(diff[:], acc[:], a2_sb[:, :, cols], ALU.subtract)
             th = work.tile([P, CH, 4], F32, name="th")
-            nc.scalar.activation(th[:], diff[:], ACT.Tanh)
-            state[c] = (a1, th)
+            nc.scalar.activation(th[:], diff[:].rearrange("p t j -> p j t"), ACT.Tanh)
+            state["a1", c] = (acc, th)
 
-        def back(c):
-            a1, th = state[c]
+        def add_tanh(c):
+            acc, th = state["a1", c]
             total = work.tile([P, CH, 4], F32, name="total")
-            nc.vector.tensor_tensor(total[:], a1, th[:], ALU.add)
-            engine = nc.gpsimd if c < GPSIMD_CHUNKS else nc.vector
-            engine.tensor_tensor(h_bf[:, c * CH : (c + 1) * CH, :], total[:], gains[:], ALU.mult)
+            nc.vector.tensor_tensor(total[:], acc[:].rearrange("p t j -> p j t"), th[:], ALU.add)
+            state["total", c] = total
+
+        def apply_gain(c):
+            nc.vector.tensor_tensor(
+                h_bf[:, c * CH : (c + 1) * CH, :], state["total", c][:], gains[:], ALU.mult
+            )
 
         def second_stage(c0, count):
             cols = slice(c0 * CH, (c0 + count) * CH)
             quantise(h_q[:, cols], h_s[:, cols], h_bf[:, cols, :].rearrange("p j t -> p (j t)"))
             w3_q, w3_s = state["w3"]
             for n in range(3):
-                acc = bank("y_%d_%d" % (c0, n), [P, count * CH])
+                acc = far_bank("y_%d_%d" % (c0, n), [P, count * CH])
                 nc.tensor.matmul_mx(
                     out=acc[:],
                     lhsT=w3_q[:, 128 * n : 128 * (n + 1)].bitcast(FP8X4),
@@ -252,19 +259,23 @@ def tile_list_pullback_view_scores_kernel(
                 )
                 nc.scalar.copy(y_sb[n][:, cols], acc[:])
 
+        def w3_operand():
+            raw = streamed("w3_raw", [P, 4, N], F32)
+            rows = w3.rearrange("(m t s) n -> t m s n", t=4, s=4)
+            for t in range(4):
+                nc.sync.dma_start(out=raw[:, t, :], in_=rows[t])
+            state["w3"] = round_and_quantise("w3", raw)
+
         def view_operands(a):
-            if a == 0:
-                state["wv0"] = plain_weight("wv0", wv, 0, nc.scalar.copy, 3)
-            else:
-                state["wv1"] = plain_weight("wv1", wv, 1, nc.scalar.copy, 3)
+            state["wv", a] = round_and_quantise("wv%d" % a, load_rows("wv_raw%d" % a, wv, a, N, 1))
             win = load_words("tab2_win%d" % a, tab2_words, a, T2)
             nc.vector.tensor_copy(v2_words[a][:], win[:].indirect(idx2[:]))
 
         def view_scores():
             for n in range(3):
-                acc = bank("b_%d" % n, [P, V])
+                acc = far_bank("b_%d" % n, [P, V])
                 for a in range(2):
-                    codes, scales = state["wv%d" % a]
+                    codes, scales = state["wv", a]
                     nc.tensor.matmul_mx(
                         out=acc[:],
                         lhsT=codes[:, 128 * n : 128 * (n + 1)].bitcast(FP8X4),
@@ -277,23 +288,29 @@ def tile_list_pullback_view_scores_kernel(
                 nc.scalar.copy(b_sb[n][:], acc[:])
 
         ends = {c0 + count - 1: (c0, count) for c0, count in GROUPS}
-        for step in range(NCH + 2):
+        for step in range(NCH + 3):
             if step < NCH:
-                front(step)
-            if 1 <= step <= NCH:
-                back(step - 1)
+                difference(step)
+            if 0 <= step - 1 < NCH:
+                add_tanh(step - 1)
+            if step - 3 in ends:
+                second_stage(*ends[step - 3])
+            if 0 <= step - 2 < NCH:
+                apply_gain(step - 2)
             if step == 1:
-                state["w3"] = plain_weight("w3", w3, 0, nc.scalar.copy, 3)
+                w3_operand()
             if step == 3:
                 view_operands(0)
             if step == 5:
                 view_operands(1)
             if step == 6:
                 view_scores()
-            if step - 2 in ends:
-                second_stage(*ends[step - 2])
 
-        for n in range(3):
-            res = held("res%d" % n, [P, V], F32)
-            nc.vector.tensor_tensor(res[:], y_sb[n][:].indirect(pick[:]), b_sb[n][:], ALU.mult)
-            nc.sync.dma_start(out=out[128 * n : 128 * (n + 1), :], in_=res[:])
+        for n, pieces in ((0, 1), (1, 1), (2, 2)):
+            width = V // pieces
+            for u in range(pieces):
+                cols = slice(u * width, (u + 1) * width)
+                res = held("res%d_%d" % (n, u), [P, width], F32)
+                entries = pick[:, u * width // 16 : (u + 1) * width // 16]
+                nc.vector.tensor_tensor(res[:], y_sb[n][:].indirect(entries), b_sb[n][:, cols], ALU.mult)
+                nc.sync.dma_start(out=out[128 * n : 128 * (n + 1), cols], in_=res[:])

@@ -20,7 +20,7 @@ ACT = mybir.ActivationFunctionType
 P = 128
 CH = 128
 NCH = S // CH
-GROUPS = ((0, 2), (2, 2), (4, 2), (6, 1), (7, 1))
+GPSIMD_CHUNKS = 6
 SC_V, SC_W2, SC_V2, SC_ALL = 0, S, S + H, S + H + V
 
 
@@ -78,12 +78,9 @@ def tile_list_pullback_view_scores_kernel(
         ts_win = held("ts_win", [P, T], U8)
         t2s_win = held("t2s_win", [P, T2], U8)
         w2s_raw = held("w2s_raw", [P, H], U8)
-        gain_rows = held("gain_rows", [P, P], F32)
         planes = [held("plane%d" % a, [P, SC_ALL], U8) for a in range(2)]
         nc.vector.memset(ts_win[0:96, :].bitcast(I32), 0)
         nc.vector.memset(t2s_win[0:96, :].bitcast(I32), 0)
-        nc.vector.memset(gain_rows[0:96, :], 0.0)
-        nc.vector.memset(gain_rows[96:124, :], 0.0)
         for a in range(2):
             nc.vector.memset(planes[a][:].bitcast(I32), 0)
 
@@ -92,24 +89,12 @@ def tile_list_pullback_view_scores_kernel(
         nc.sync.dma_start(idx2[:], offs2)
         load_scale_rows(t2s_win, tab2_scales)
         load_scale_rows(w2s_raw, w2_scales)
-        nc.sync.dma_start(
-            out=gain_rows[124:128, :], in_=gain.rearrange("(m t s) -> t m s", t=4, s=4)
-        )
         w2_raw = streamed("w2_raw", [P, 2, 2 * H], U8)
         nc.sync.dma_start(
             out=w2_raw[:].bitcast(I32), in_=w2_words.rearrange("a p n -> p a n").bitcast(I32)
         )
         tab_win = [load_words("tab_win%d" % a, tab_words, a, T) for a in range(2)]
         nc.sync.dma_start(pick[:], pos1)
-
-        ident = held("ident", [P, P], F32)
-        make_identity(nc, ident[:])
-        gain_cols = far_bank("gain_cols", [P, P])
-        nc.tensor.transpose(gain_cols[:], gain_rows[:], ident[:])
-        gains = held("gains", [P, CH, 4], F32)
-        nc.scalar.activation(
-            gains[:], gain_cols[:, 124:128].unsqueeze(1).to_broadcast([P, CH, 4]), ACT.Copy
-        )
 
         vs_g = held("vs_g", [P, S], U8)
         v2s_g = held("v2s_g", [P, V], U8)
@@ -168,7 +153,8 @@ def tile_list_pullback_view_scores_kernel(
             )
             for t in range(4):
                 a2_pass(half, t, 1)
-                nc.scalar.copy(a2_sb[:, t, cols], a2_acc[half, t][:])
+                if half == 0:
+                    nc.scalar.copy(a2_sb[:, t, cols], a2_acc[half, t][:])
 
         w1_bf = [held("w1_bf%d" % a, [P, 4, P, 4], BF16) for a in range(2)]
         w1_q = [held("w1_q%d" % a, [P, H], U32) for a in range(2)]
@@ -191,24 +177,31 @@ def tile_list_pullback_view_scores_kernel(
                 w1_bf[1][:, 2 * u : 2 * u + 2].rearrange("p t m i -> p (t m i)"),
             )
 
-        def round_and_quantise(name, raw):
+        ident = held("ident", [P, P], F32)
+        make_identity(nc, ident[:])
+        gain_rows = streamed("gain_rows", [P, P], F32)
+        nc.gpsimd.memset(gain_rows[0:96, :], 0.0)
+        nc.gpsimd.memset(gain_rows[96:124, :], 0.0)
+        nc.sync.dma_start(
+            out=gain_rows[124:128, :], in_=gain.rearrange("(m t s) -> t m s", t=4, s=4)
+        )
+        gain_cols = far_bank("gain_cols", [P, P])
+        nc.tensor.transpose(gain_cols[:], gain_rows[:], ident[:])
+        gains = held("gains", [P, CH, 4], F32)
+        nc.scalar.activation(
+            gains[:], gain_cols[:, 124:128].unsqueeze(1).to_broadcast([P, CH, 4]), ACT.Copy
+        )
+
+        def round_plain(name, raw):
             rounded = held(name + "_bf", [P, N, 4], BF16)
-            codes = held(name + "_q", [P, N], U32)
-            scales = held(name + "_s", [P, N], U8)
             for c0 in range(0, N, P):
                 nc.scalar.copy(
                     rounded[:, c0 : c0 + P, :].rearrange("p (c s) i -> p c i s", s=4),
                     raw[:, :, c0 : c0 + P].rearrange("p i (c s) -> p c i s", s=4),
                 )
-            quantise(codes[:], scales[:], rounded[:].rearrange("p c i -> p (c i)"))
-            return codes, scales
+            return rounded
 
         h_bf = held("h_bf", [P, S, 4], BF16)
-        h_q = held("h_q", [P, S], U32)
-        h_s = held("h_s", [P, S], U8)
-        y_sb = [held("y_sb%d" % n, [P, S], F32) for n in range(3)]
-        b_sb = [held("b_sb%d" % n, [P, V], F32) for n in range(3)]
-        v2_words = [held("v2_words%d" % a, [P, V], U32) for a in range(2)]
         state = {}
 
         def difference(c):
@@ -231,86 +224,111 @@ def tile_list_pullback_view_scores_kernel(
             nc.scalar.activation(th[:], diff[:].rearrange("p t j -> p j t"), ACT.Tanh)
             state["a1", c] = (acc, th)
 
+        def summed(name, shape, dtype):
+            return work.tile(shape, dtype, name=name, tag="summed", bufs=2, align_bytes=64)
+
         def add_tanh(c):
             acc, th = state["a1", c]
-            total = work.tile([P, CH, 4], F32, name="total")
-            nc.vector.tensor_tensor(total[:], acc[:].rearrange("p t j -> p j t"), th[:], ALU.add)
-            state["total", c] = total
+            if c < GPSIMD_CHUNKS:
+                total = summed("total%d" % c, [P, CH, 4], F32)[:]
+            else:
+                if c == GPSIMD_CHUNKS:
+                    state["last"] = held("last_totals", [P, NCH - GPSIMD_CHUNKS, CH, 4], F32)
+                total = state["last"][:, c - GPSIMD_CHUNKS]
+            nc.vector.tensor_tensor(total, acc[:].rearrange("p t j -> p j t"), th[:], ALU.add)
+            if c < GPSIMD_CHUNKS:
+                nc.gpsimd.tensor_tensor(h_bf[:, c * CH : (c + 1) * CH, :], total, gains[:], ALU.mult)
 
-        def apply_gain(c):
-            nc.vector.tensor_tensor(
-                h_bf[:, c * CH : (c + 1) * CH, :], state["total", c][:], gains[:], ALU.mult
-            )
-
-        def second_stage(c0, count):
-            cols = slice(c0 * CH, (c0 + count) * CH)
-            quantise(h_q[:, cols], h_s[:, cols], h_bf[:, cols, :].rearrange("p j t -> p (j t)"))
-            w3_q, w3_s = state["w3"]
-            for n in range(3):
-                acc = far_bank("y_%d_%d" % (c0, n), [P, count * CH])
-                nc.tensor.matmul_mx(
-                    out=acc[:],
-                    lhsT=w3_q[:, 128 * n : 128 * (n + 1)].bitcast(FP8X4),
-                    lhsT_scale=w3_s[:, 128 * n : 128 * (n + 1)],
-                    rhs=h_q[:, cols].bitcast(FP8X4),
-                    rhs_scale=h_s[:, cols],
-                    start=True,
-                    stop=True,
-                )
-                nc.scalar.copy(y_sb[n][:, cols], acc[:])
-
-        def w3_operand():
-            raw = streamed("w3_raw", [P, 4, N], F32)
-            rows = w3.rearrange("(m t s) n -> t m s n", t=4, s=4)
-            for t in range(4):
-                nc.sync.dma_start(out=raw[:, t, :], in_=rows[t])
-            state["w3"] = round_and_quantise("w3", raw)
-
-        def view_operands(a):
-            state["wv", a] = round_and_quantise("wv%d" % a, load_rows("wv_raw%d" % a, wv, a, N, 1))
-            win = load_words("tab2_win%d" % a, tab2_words, a, T2)
-            nc.vector.tensor_copy(v2_words[a][:], win[:].indirect(idx2[:]))
-
-        def view_scores():
-            for n in range(3):
-                acc = far_bank("b_%d" % n, [P, V])
-                for a in range(2):
-                    codes, scales = state["wv", a]
-                    nc.tensor.matmul_mx(
-                        out=acc[:],
-                        lhsT=codes[:, 128 * n : 128 * (n + 1)].bitcast(FP8X4),
-                        lhsT_scale=scales[:, 128 * n : 128 * (n + 1)],
-                        rhs=v2_words[a][:].bitcast(FP8X4),
-                        rhs_scale=planes[a][:, SC_V2:SC_ALL],
-                        start=(a == 0),
-                        stop=(a == 1),
-                    )
-                nc.scalar.copy(b_sb[n][:], acc[:])
-
-        ends = {c0 + count - 1: (c0, count) for c0, count in GROUPS}
-        for step in range(NCH + 3):
+        for step in range(NCH + 1):
             if step < NCH:
                 difference(step)
-            if 0 <= step - 1 < NCH:
+            if step < 2:
+                for t in (2 * step, 2 * step + 1):
+                    nc.scalar.copy(a2_sb[:, t, 512:S], a2_acc[1, t][:])
+            if step >= 1:
                 add_tanh(step - 1)
-            if step - 3 in ends:
-                second_stage(*ends[step - 3])
-            if 0 <= step - 2 < NCH:
-                apply_gain(step - 2)
-            if step == 1:
-                w3_operand()
-            if step == 3:
-                view_operands(0)
-            if step == 5:
-                view_operands(1)
-            if step == 6:
-                view_scores()
+            if step == 2:
+                w3_raw = streamed("w3_raw", [P, 4, N], F32)
+                w3_rows = w3.rearrange("(m t s) n -> t m s n", t=4, s=4)
+                for t in range(4):
+                    nc.sync.dma_start(out=w3_raw[:, t, :], in_=w3_rows[t])
+                w3_bf = round_plain("w3", w3_raw)
+            if step in (3, 5):
+                a = (step - 3) // 2
+                state["wv", a] = round_plain("wv%d" % a, load_rows("wv_raw%d" % a, wv, a, N, 1))
+                state["win", a] = load_words("tab2_win%d" % a, tab2_words, a, T2)
 
-        for n, pieces in ((0, 1), (1, 1), (2, 2)):
-            width = V // pieces
-            for u in range(pieces):
-                cols = slice(u * width, (u + 1) * width)
-                res = held("res%d_%d" % (n, u), [P, width], F32)
-                entries = pick[:, u * width // 16 : (u + 1) * width // 16]
-                nc.vector.tensor_tensor(res[:], y_sb[n][:].indirect(entries), b_sb[n][:, cols], ALU.mult)
-                nc.sync.dma_start(out=out[128 * n : 128 * (n + 1), cols], in_=res[:])
+        v2_words = summed("v2_words", [P, 2, V], U32)
+        codes = summed("codes", [P, S + 3 * N], U32)
+        scales = held("scales", [P, S + 3 * N], U8)
+        w3_cols = slice(S, S + N)
+        wv_cols = [slice(S + (1 + a) * N, S + (2 + a) * N) for a in range(2)]
+
+        def stationary(cols, n):
+            part = slice(cols.start + 128 * n, cols.start + 128 * (n + 1))
+            return codes[:, part].bitcast(FP8X4), scales[:, part]
+
+        y_sb = [held("y_sb%d" % n, [P, S], F32) for n in range(3)]
+        b_sb = [held("b_sb%d" % n, [P, V], F32) for n in range(3)]
+        quantise(codes[:, w3_cols], scales[:, w3_cols], w3_bf[:].rearrange("p c i -> p (c i)"))
+
+        def quantise_h(c0, c1):
+            cols = slice(c0 * CH, c1 * CH)
+            quantise(codes[:, cols], scales[:, cols], h_bf[:, cols, :].rearrange("p j t -> p (j t)"))
+
+        def segment_scores(c0, c1, n):
+            cols = slice(c0 * CH, c1 * CH)
+            acc = far_bank("y_%d_%d" % (c0, n), [P, (c1 - c0) * CH])
+            lhs, lhs_scale = stationary(w3_cols, n)
+            nc.tensor.matmul_mx(
+                out=acc[:],
+                lhsT=lhs,
+                lhsT_scale=lhs_scale,
+                rhs=codes[:, cols].bitcast(FP8X4),
+                rhs_scale=scales[:, cols],
+                start=True,
+                stop=True,
+            )
+            nc.scalar.copy(y_sb[n][:, cols], acc[:])
+
+        for c0, c1 in ((0, 4), (4, GPSIMD_CHUNKS)):
+            quantise_h(c0, c1)
+            for n in range(3):
+                segment_scores(c0, c1, n)
+
+        for a in range(2):
+            nc.vector.tensor_copy(v2_words[:, a, :], state["win", a][:].indirect(idx2[:]))
+            quantise(
+                codes[:, wv_cols[a]], scales[:, wv_cols[a]],
+                state["wv", a][:].rearrange("p c i -> p (c i)"),
+            )
+        rest = NCH - GPSIMD_CHUNKS
+        nc.vector.tensor_tensor(
+            h_bf[:, GPSIMD_CHUNKS * CH :, :].rearrange("p (c j) t -> p c (j t)", c=rest),
+            state["last"][:].rearrange("p c j t -> p c (j t)"),
+            gains[:].rearrange("p j t -> p (j t)").unsqueeze(1).to_broadcast([P, rest, 4 * CH]),
+            ALU.mult,
+        )
+
+        quantise_h(GPSIMD_CHUNKS, NCH)
+
+        for n in range(3):
+            acc = near_bank("b_%d" % n, [P, V])
+            for a in range(2):
+                lhs, lhs_scale = stationary(wv_cols[a], n)
+                nc.tensor.matmul_mx(
+                    out=acc[:],
+                    lhsT=lhs,
+                    lhsT_scale=lhs_scale,
+                    rhs=v2_words[:, a, :].bitcast(FP8X4),
+                    rhs_scale=planes[a][:, SC_V2:SC_ALL],
+                    start=(a == 0),
+                    stop=(a == 1),
+                )
+            nc.scalar.copy(b_sb[n][:], acc[:])
+            segment_scores(GPSIMD_CHUNKS, NCH, n)
+
+        for n in range(3):
+            res = held("res%d" % n, [P, V], F32)
+            nc.vector.tensor_tensor(res[:], y_sb[n][:].indirect(pick[:]), b_sb[n][:], ALU.mult)
+            nc.sync.dma_start(out=out[128 * n : 128 * (n + 1), :], in_=res[:])

@@ -123,38 +123,47 @@ def tile_list_pullback_view_scores_kernel(
         w1_raw = [load_rows("w1_raw0", w1, 0, H, 1), load_rows("w1_raw1", w1, 1, H, 2)]
 
         v_words = [held("v_words%d" % a, [P, S], U32) for a in range(2)]
-        a2_sb = held("a2_sb", [P, 4, S], F32)
-        a2_acc = {}
-        for half in range(2):
-            for t in range(4):
-                place = near_bank if 4 * half + t < 3 else far_bank
-                a2_acc[half, t] = place("a2_%d_%d" % (half, t), [P, 512])
 
-        def a2_pass(half, t, a):
-            cols = slice(512 * half, 512 * (half + 1))
-            nc.tensor.matmul_mx(
-                out=a2_acc[half, t][:],
-                lhsT=w2_perm[:, a, 256 * t : 256 * (t + 1)].bitcast(FP4X4),
-                lhsT_scale=planes[a][:, SC_W2 + 128 * t : SC_W2 + 128 * (t + 1)],
-                rhs=v_words[a][:, cols].bitcast(FP8X4),
-                rhs_scale=planes[a][:, cols],
-                start=(a == 0),
-                stop=(a == 1),
+        def first_stage_pass(acc, c, a, stationary_of):
+            cols = slice(c * CH, (c + 1) * CH)
+            for t in range(4):
+                lhs, lhs_scale = stationary_of(a, t)
+                nc.tensor.matmul_mx(
+                    out=acc[:, t, :],
+                    lhsT=lhs,
+                    lhsT_scale=lhs_scale,
+                    rhs=v_words[a][:, cols].bitcast(FP8X4),
+                    rhs_scale=planes[a][:, cols],
+                    start=(a == 0 and t == 0),
+                    stop=(a == 1 and t == 3),
+                )
+
+        def w2_columns(a, t):
+            return (
+                w2_perm[:, a, 256 * t : 256 * (t + 1)].bitcast(FP4X4),
+                planes[a][:, SC_W2 + 128 * t : SC_W2 + 128 * (t + 1)],
             )
+
+        a2_acc = [
+            (near_bank if c < 3 else far_bank)("a2_%d" % c, [P, 4, CH]) for c in range(NCH)
+        ]
+        a2_sb = [held("a2_sb%d" % c, [P, CH, 4], F32) for c in range(NCH)]
+
+        def copy_a2(c):
+            nc.scalar.copy(a2_sb[c][:], a2_acc[c][:].rearrange("p t j -> p j t"))
 
         nc.vector.tensor_copy(v_words[0][:], tab_win[0][:].indirect(idx[:]))
+        for c in range(NCH):
+            first_stage_pass(a2_acc[c], c, 0, w2_columns)
         for half in range(2):
-            for t in range(4):
-                a2_pass(half, t, 0)
-        for half in range(2):
-            cols = slice(512 * half, 512 * (half + 1))
             nc.vector.tensor_copy(
-                v_words[1][:, cols], tab_win[1][:].indirect(idx[:, 32 * half : 32 * (half + 1)])
+                v_words[1][:, 512 * half : 512 * (half + 1)],
+                tab_win[1][:].indirect(idx[:, 32 * half : 32 * (half + 1)]),
             )
-            for t in range(4):
-                a2_pass(half, t, 1)
-                if half == 0:
-                    nc.scalar.copy(a2_sb[:, t, cols], a2_acc[half, t][:])
+            for c in range(4 * half, 4 * half + 4):
+                first_stage_pass(a2_acc[c], c, 1, w2_columns)
+        for c in range(4):
+            copy_a2(c)
 
         w1_bf = [held("w1_bf%d" % a, [P, 4, P, 4], BF16) for a in range(2)]
         w1_q = [held("w1_q%d" % a, [P, H], U32) for a in range(2)]
@@ -162,8 +171,8 @@ def tile_list_pullback_view_scores_kernel(
 
         def round_w1(a, c0, c1):
             nc.vector.tensor_copy(
-                w1_bf[a][:, :, c0 // 4 : c1 // 4, :].rearrange("p t (m s) i -> p t m i s", s=4),
-                w1_raw[a][:, :, c0:c1].rearrange("p i (m t s) -> p t m i s", t=4, s=4),
+                w1_bf[a][:, :, c0 // 4 : c1 // 4, :].rearrange("p t (m s) i -> p t m s i", s=4),
+                w1_raw[a][:, :, c0:c1].rearrange("p i (m t s) -> p t m s i", t=4, s=4),
             )
 
         round_w1(0, 0, H)
@@ -196,63 +205,59 @@ def tile_list_pullback_view_scores_kernel(
             rounded = held(name + "_bf", [P, N, 4], BF16)
             for c0 in range(0, N, P):
                 nc.scalar.copy(
-                    rounded[:, c0 : c0 + P, :].rearrange("p (c s) i -> p c i s", s=4),
-                    raw[:, :, c0 : c0 + P].rearrange("p i (c s) -> p c i s", s=4),
+                    rounded[:, c0 : c0 + P, :], raw[:, :, c0 : c0 + P].rearrange("p i c -> p c i")
                 )
             return rounded
 
         h_bf = held("h_bf", [P, S, 4], BF16)
         state = {}
 
+        def w1_columns(a, t):
+            cols = slice(128 * t, 128 * (t + 1))
+            return w1_q[a][:, cols].bitcast(FP8X4), w1_s[a][:, cols]
+
         def difference(c):
-            cols = slice(c * CH, (c + 1) * CH)
             acc = near_bank("a1_%d" % c, [P, 4, CH])
             for a in range(2):
-                for t in range(4):
-                    nc.tensor.matmul_mx(
-                        out=acc[:, t, :],
-                        lhsT=w1_q[a][:, 128 * t : 128 * (t + 1)].bitcast(FP8X4),
-                        lhsT_scale=w1_s[a][:, 128 * t : 128 * (t + 1)],
-                        rhs=v_words[a][:, cols].bitcast(FP8X4),
-                        rhs_scale=planes[a][:, cols],
-                        start=(a == 0 and t == 0),
-                        stop=(a == 1 and t == 3),
-                    )
-            diff = work.tile([P, 4, CH], F32, name="diff")
-            nc.vector.tensor_tensor(diff[:], acc[:], a2_sb[:, :, cols], ALU.subtract)
+                first_stage_pass(acc, c, a, w1_columns)
+            a1 = acc[:].rearrange("p t j -> p j t")
+            diff = work.tile([P, CH, 4], F32, name="diff")
+            nc.vector.tensor_tensor(diff[:], a1, a2_sb[c][:], ALU.subtract)
             th = work.tile([P, CH, 4], F32, name="th")
-            nc.scalar.activation(th[:], diff[:].rearrange("p t j -> p j t"), ACT.Tanh)
-            state["a1", c] = (acc, th)
+            nc.scalar.activation(th[:], diff[:], ACT.Tanh)
+            state["a1", c] = (a1, th)
 
         def summed(name, shape, dtype):
             return work.tile(shape, dtype, name=name, tag="summed", bufs=2, align_bytes=64)
 
         def add_tanh(c):
-            acc, th = state["a1", c]
+            a1, th = state["a1", c]
             if c < GPSIMD_CHUNKS:
                 total = summed("total%d" % c, [P, CH, 4], F32)[:]
             else:
                 if c == GPSIMD_CHUNKS:
                     state["last"] = held("last_totals", [P, NCH - GPSIMD_CHUNKS, CH, 4], F32)
                 total = state["last"][:, c - GPSIMD_CHUNKS]
-            nc.vector.tensor_tensor(total, acc[:].rearrange("p t j -> p j t"), th[:], ALU.add)
+            nc.vector.tensor_tensor(total, a1, th[:], ALU.add)
             if c < GPSIMD_CHUNKS:
                 nc.gpsimd.tensor_tensor(h_bf[:, c * CH : (c + 1) * CH, :], total, gains[:], ALU.mult)
+
+        w3_raw = streamed("w3_raw", [P, 4, N], F32)
+        w3_rows = w3.rearrange("(m t s) n -> t m s n", t=4, s=4)
+        for t in range(4):
+            nc.sync.dma_start(out=w3_raw[:, t, :], in_=w3_rows[t])
+        w3_bf = held("w3_bf", [P, N, 4], BF16)
+        nc.gpsimd.tensor_scalar(
+            w3_bf[:], w3_raw[:].rearrange("p i c -> p c i"), 1.0, 0.0, ALU.mult, ALU.add
+        )
 
         for step in range(NCH + 1):
             if step < NCH:
                 difference(step)
-            if step < 2:
-                for t in (2 * step, 2 * step + 1):
-                    nc.scalar.copy(a2_sb[:, t, 512:S], a2_acc[1, t][:])
+            if step < 4:
+                copy_a2(step + 4)
             if step >= 1:
                 add_tanh(step - 1)
-            if step == 2:
-                w3_raw = streamed("w3_raw", [P, 4, N], F32)
-                w3_rows = w3.rearrange("(m t s) n -> t m s n", t=4, s=4)
-                for t in range(4):
-                    nc.sync.dma_start(out=w3_raw[:, t, :], in_=w3_rows[t])
-                w3_bf = round_plain("w3", w3_raw)
             if step in (3, 5):
                 a = (step - 3) // 2
                 state["wv", a] = round_plain("wv%d" % a, load_rows("wv_raw%d" % a, wv, a, N, 1))

from contextlib import ExitStack

import concourse.mybir as mybir
from concourse.masks import make_identity

K, T, S, H, N, K2, T2, V = 1024, 4096, 1024, 512, 384, 1024, 2048, 512
FLOPS = 2 * (2 * K * H * S + H * N * S + K2 * N * V)

F32 = mybir.dt.float32
BF16 = mybir.dt.bfloat16
I32 = mybir.dt.int32
U32 = mybir.dt.uint32
U16 = mybir.dt.uint16
U8 = mybir.dt.uint8
FP8X4 = mybir.dt.float8_e4m3fn_x4
FP4X4 = mybir.dt.float4_e2m1fn_x4
ALU = mybir.AluOpType
ACT = mybir.ActivationFunctionType

P = 128
CH = 128
NCH = S // CH
GPSIMD_CHUNKS = 6
SC_V, SC_W2, SC_V2, SC_ALL = 0, S, S + H, S + H + V


def tile_list_pullback_view_scores_kernel(
    tc, tab_words, tab_scales, tab2_words, tab2_scales, offs, offs2, pos1,
    w1, w2_words, w2_scales, gain, w3, wv, out,
):
    nc = tc.nc
    with ExitStack() as ctx:
        keep = ctx.enter_context(tc.tile_pool(name="keep", bufs=1))
        stream = ctx.enter_context(tc.tile_pool(name="stream", bufs=3))
        work = ctx.enter_context(tc.tile_pool(name="work", bufs=3))
        psum = ctx.enter_context(tc.psum_pool(name="psum", bufs=1))

        def held(name, shape, dtype):
            return keep.tile(shape, dtype, name=name, align_bytes=64)

        def streamed(name, shape, dtype):
            return stream.tile(shape, dtype, name=name, tag="stream", align_bytes=64)

        def near_bank(name, shape):
            return psum.tile(shape, F32, name=name, tag="near", bufs=3)

        def far_bank(name, shape):
            return psum.tile(shape, F32, name=name, tag="far", bufs=5)

        def quantise(codes, scales, values):
            nc.vector.quantize_mx(out=codes.bitcast(FP8X4), scales=scales, in_=values)

        def load_scale_rows(tile, rows):
            nc.sync.dma_start(
                out=tile[96:128, :].bitcast(I32),
                in_=rows.rearrange("a q n -> (a q) n").bitcast(I32),
            )

        def load_words(name, words, a, cols):
            win = streamed(name, [P, cols], U32)
            nc.sync.dma_start(
                out=win[:].bitcast(I32),
                in_=words[a].rearrange("p n t -> p (n t)").bitcast(I32),
            )
            return win

        def load_rows(name, w, a, cols, pieces):
            raw = streamed(name, [P, 4, cols], F32)
            rows = w[512 * a : 512 * (a + 1), :].rearrange("(p i) c -> p i c", i=4)
            step = cols // pieces
            for c0 in range(0, cols, step):
                nc.sync.dma_start(out=raw[:, :, c0 : c0 + step], in_=rows[:, :, c0 : c0 + step])
            return raw

        idx = keep.tile([P, S // 16], U16, name="idx")
        idx2 = keep.tile([P, V // 16], U16, name="idx2")
        pick = keep.tile([P, V // 16], U16, name="pick")
        ts_win = held("ts_win", [P, T], U8)
        t2s_win = held("t2s_win", [P, T2], U8)
        w2s_raw = held("w2s_raw", [P, H], U8)
        planes = [held("plane%d" % a, [P, SC_ALL], U8) for a in range(2)]
        nc.vector.memset(ts_win[0:96, :].bitcast(I32), 0)
        nc.vector.memset(t2s_win[0:96, :].bitcast(I32), 0)
        for a in range(2):
            nc.vector.memset(planes[a][:].bitcast(I32), 0)

        nc.sync.dma_start(idx[:], offs)
        load_scale_rows(ts_win, tab_scales)
        nc.sync.dma_start(idx2[:], offs2)
        load_scale_rows(t2s_win, tab2_scales)
        load_scale_rows(w2s_raw, w2_scales)
        w2_raw = streamed("w2_raw", [P, 2, 2 * H], U8)
        nc.sync.dma_start(
            out=w2_raw[:].bitcast(I32), in_=w2_words.rearrange("a p n -> p a n").bitcast(I32)
        )
        tab_win = [load_words("tab_win%d" % a, tab_words, a, T) for a in range(2)]
        nc.sync.dma_start(pick[:], pos1)

        vs_g = held("vs_g", [P, S], U8)
        v2s_g = held("v2s_g", [P, V], U8)
        staged = held("staged", [P, SC_ALL], U8)
        nc.vector.tensor_copy(vs_g[:], ts_win[:].indirect(idx[:]))
        nc.vector.tensor_copy(v2s_g[:], t2s_win[:].indirect(idx2[:]))
        nc.vector.tensor_copy(staged[96:128, SC_V:SC_W2].bitcast(I32), vs_g[96:128, :].bitcast(I32))
        nc.vector.tensor_copy(
            staged[96:128, SC_W2:SC_V2].bitcast(I32).rearrange("p (t m) -> p t m", t=4),
            w2s_raw[96:128, :].bitcast(I32).rearrange("p (m t) -> p t m", t=4),
        )
        nc.vector.tensor_copy(staged[96:128, SC_V2:SC_ALL].bitcast(I32), v2s_g[96:128, :].bitcast(I32))
        for a in range(2):
            for q in range(4):
                row = 96 + 16 * a + 4 * q
                nc.scalar.dma_start(
                    out=planes[a][32 * q : 32 * q + 4, :].bitcast(I32),
                    in_=staged[row : row + 4, :].bitcast(I32),
                )

        w2_perm = held("w2_perm", [P, 2, 2 * H], U8)
        nc.vector.tensor_copy(
            w2_perm[:].bitcast(I32).rearrange("p a (t m w) -> p a t m w", t=4, w=2),
            w2_raw[:].bitcast(I32).rearrange("p a (m t w) -> p a t m w", t=4, w=2),
        )
        w1_raw = [load_rows("w1_raw0", w1, 0, H, 1), load_rows("w1_raw1", w1, 1, H, 2)]

        v_words = [held("v_words%d" % a, [P, S], U32) for a in range(2)]

        def first_stage_pass(acc, c, a, stationary_of):
            cols = slice(c * CH, (c + 1) * CH)
            for t in range(4):
                lhs, lhs_scale = stationary_of(a, t)
                nc.tensor.matmul_mx(
                    out=acc[:, t, :],
                    lhsT=lhs,
                    lhsT_scale=lhs_scale,
                    rhs=v_words[a][:, cols].bitcast(FP8X4),
                    rhs_scale=planes[a][:, cols],
                    start=(a == 0 and t == 0),
                    stop=(a == 1 and t == 3),
                )

        def w2_columns(a, t):
            return (
                w2_perm[:, a, 256 * t : 256 * (t + 1)].bitcast(FP4X4),
                planes[a][:, SC_W2 + 128 * t : SC_W2 + 128 * (t + 1)],
            )

        a2_acc = [
            (near_bank if c < 3 else far_bank)("a2_%d" % c, [P, 4, CH]) for c in range(NCH)
        ]
        a2_sb = [held("a2_sb%d" % c, [P, CH, 4], F32) for c in range(NCH)]

        def copy_a2(c):
            nc.scalar.copy(a2_sb[c][:], a2_acc[c][:].rearrange("p t j -> p j t"))

        nc.vector.tensor_copy(v_words[0][:], tab_win[0][:].indirect(idx[:]))
        for c in range(NCH):
            first_stage_pass(a2_acc[c], c, 0, w2_columns)
        for half in range(2):
            nc.vector.tensor_copy(
                v_words[1][:, 512 * half : 512 * (half + 1)],
                tab_win[1][:].indirect(idx[:, 32 * half : 32 * (half + 1)]),
            )
            for c in range(4 * half, 4 * half + 4):
                first_stage_pass(a2_acc[c], c, 1, w2_columns)
        for c in range(4):
            copy_a2(c)

        w1_bf = [held("w1_bf%d" % a, [P, 4, P, 4], BF16) for a in range(2)]
        w1_q = [held("w1_q%d" % a, [P, H], U32) for a in range(2)]
        w1_s = [held("w1_s%d" % a, [P, H], U8) for a in range(2)]

        def round_w1(a, c0, c1):
            nc.vector.tensor_copy(
                w1_bf[a][:, :, c0 // 4 : c1 // 4, :].rearrange("p t (m s) i -> p t m s i", s=4),
                w1_raw[a][:, :, c0:c1].rearrange("p i (m t s) -> p t m s i", t=4, s=4),
            )

        round_w1(0, 0, H)
        quantise(w1_q[0][:], w1_s[0][:], w1_bf[0][:].rearrange("p t m i -> p (t m i)"))
        round_w1(1, 0, H // 2)
        round_w1(1, H // 2, H)
        for u in range(2):
            quantise(
                w1_q[1][:, 256 * u : 256 * (u + 1)],
                w1_s[1][:, 256 * u : 256 * (u + 1)],
                w1_bf[1][:, 2 * u : 2 * u + 2].rearrange("p t m i -> p (t m i)"),
            )

        ident = held("ident", [P, P], F32)
        make_identity(nc, ident[:])
        gain_rows = streamed("gain_rows", [P, P], F32)
        nc.gpsimd.memset(gain_rows[0:96, :], 0.0)
        nc.gpsimd.memset(gain_rows[96:124, :], 0.0)
        nc.sync.dma_start(
            out=gain_rows[124:128, :], in_=gain.rearrange("(m t s) -> t m s", t=4, s=4)
        )
        gain_cols = far_bank("gain_cols", [P, P])
        nc.tensor.transpose(gain_cols[:], gain_rows[:], ident[:])
        gains = held("gains", [P, CH, 4], F32)
        nc.scalar.activation(
            gains[:], gain_cols[:, 124:128].unsqueeze(1).to_broadcast([P, CH, 4]), ACT.Copy
        )

        def round_plain(name, raw):
            rounded = held(name + "_bf", [P, N, 4], BF16)
            for c0 in range(0, N, P):
                nc.scalar.copy(
                    rounded[:, c0 : c0 + P, :], raw[:, :, c0 : c0 + P].rearrange("p i c -> p c i")
                )
            return rounded

        h_bf = held("h_bf", [P, S, 4], BF16)
        state = {}

        def w1_columns(a, t):
            cols = slice(128 * t, 128 * (t + 1))
            return w1_q[a][:, cols].bitcast(FP8X4), w1_s[a][:, cols]

        def difference(c):
            acc = near_bank("a1_%d" % c, [P, 4, CH])
            for a in range(2):
                first_stage_pass(acc, c, a, w1_columns)
            a1 = acc[:].rearrange("p t j -> p j t")
            diff = work.tile([P, CH, 4], F32, name="diff")
            nc.vector.tensor_tensor(diff[:], a1, a2_sb[c][:], ALU.subtract)
            th = work.tile([P, CH, 4], F32, name="th")
            nc.scalar.activation(th[:], diff[:], ACT.Tanh)
            state["a1", c] = (a1, th)

        def summed(name, shape, dtype):
            return work.tile(shape, dtype, name=name, tag="summed", bufs=2, align_bytes=64)

        def add_tanh(c):
            a1, th = state["a1", c]
            if c < GPSIMD_CHUNKS:
                total = summed("total%d" % c, [P, CH, 4], F32)[:]
            else:
                if c == GPSIMD_CHUNKS:
                    state["last"] = held("last_totals", [P, NCH - GPSIMD_CHUNKS, CH, 4], F32)
                total = state["last"][:, c - GPSIMD_CHUNKS]
            nc.vector.tensor_tensor(total, a1, th[:], ALU.add)
            if c < GPSIMD_CHUNKS:
                nc.gpsimd.tensor_tensor(h_bf[:, c * CH : (c + 1) * CH, :], total, gains[:], ALU.mult)

        w3_raw = streamed("w3_raw", [P, 4, N], F32)
        w3_rows = w3.rearrange("(m t s) n -> t m s n", t=4, s=4)
        for t in range(4):
            nc.sync.dma_start(out=w3_raw[:, t, :], in_=w3_rows[t])
        w3_bf = held("w3_bf", [P, N, 4], BF16)
        nc.gpsimd.tensor_scalar(
            w3_bf[:], w3_raw[:].rearrange("p i c -> p c i"), 1.0, 0.0, ALU.mult, ALU.add
        )

        for step in range(NCH + 1):
            if step < NCH:
                difference(step)
            if step < 4:
                copy_a2(step + 4)
            if step >= 1:
                add_tanh(step - 1)
            if step in (3, 5):
                a = (step - 3) // 2
                state["wv", a] = round_plain("wv%d" % a, load_rows("wv_raw%d" % a, wv, a, N, 1))
                state["win", a] = load_words("tab2_win%d" % a, tab2_words, a, T2)

        v2_words = summed("v2_words", [P, 2, V], U32)
        codes = summed("codes", [P, S + 3 * N], U32)
        scales = held("scales", [P, S + 3 * N], U8)
        w3_cols = slice(S, S + N)
        wv_cols = [slice(S + (1 + a) * N, S + (2 + a) * N) for a in range(2)]

        def stationary(cols, n):
            part = slice(cols.start + 128 * n, cols.start + 128 * (n + 1))
            return codes[:, part].bitcast(FP8X4), scales[:, part]

        y_sb = [held("y_sb%d" % n, [P, S], F32) for n in range(3)]
        b_sb = [held("b_sb%d" % n, [P, V], F32) for n in range(3)]
        quantise(codes[:, w3_cols], scales[:, w3_cols], w3_bf[:].rearrange("p c i -> p (c i)"))

        def quantise_h(c0, c1):
            cols = slice(c0 * CH, c1 * CH)
            quantise(codes[:, cols], scales[:, cols], h_bf[:, cols, :].rearrange("p j t -> p (j t)"))

        def segment_scores(c0, c1, n):
            cols = slice(c0 * CH, c1 * CH)
            acc = far_bank("y_%d_%d" % (c0, n), [P, (c1 - c0) * CH])
            lhs, lhs_scale = stationary(w3_cols, n)
            nc.tensor.matmul_mx(
                out=acc[:],
                lhsT=lhs,
                lhsT_scale=lhs_scale,
                rhs=codes[:, cols].bitcast(FP8X4),
                rhs_scale=scales[:, cols],
                start=True,
                stop=True,
            )
            nc.scalar.copy(y_sb[n][:, cols], acc[:])

        for c0, c1 in ((0, 4), (4, GPSIMD_CHUNKS)):
            quantise_h(c0, c1)
            for n in range(3):
                segment_scores(c0, c1, n)

        for a in range(2):
            nc.vector.tensor_copy(v2_words[:, a, :], state["win", a][:].indirect(idx2[:]))
            quantise(
                codes[:, wv_cols[a]], scales[:, wv_cols[a]],
                state["wv", a][:].rearrange("p c i -> p (c i)"),
            )
        rest = NCH - GPSIMD_CHUNKS
        nc.vector.tensor_tensor(
            h_bf[:, GPSIMD_CHUNKS * CH :, :].rearrange("p (c j) t -> p c (j t)", c=rest),
            state["last"][:].rearrange("p c j t -> p c (j t)"),
            gains[:].rearrange("p j t -> p (j t)").unsqueeze(1).to_broadcast([P, rest, 4 * CH]),
            ALU.mult,
        )

        quantise_h(GPSIMD_CHUNKS, NCH)

        for n in range(3):
            acc = near_bank("b_%d" % n, [P, V])
            for a in range(2):
                lhs, lhs_scale = stationary(wv_cols[a], n)
                nc.tensor.matmul_mx(
                    out=acc[:],
                    lhsT=lhs,
                    lhsT_scale=lhs_scale,
                    rhs=v2_words[:, a, :].bitcast(FP8X4),
                    rhs_scale=planes[a][:, SC_V2:SC_ALL],
                    start=(a == 0),
                    stop=(a == 1),
                )
            nc.scalar.copy(b_sb[n][:], acc[:])
            segment_scores(GPSIMD_CHUNKS, NCH, n)

        for n in range(3):
            res = held("res%d" % n, [P, V], F32)
            nc.vector.tensor_tensor(res[:], y_sb[n][:].indirect(pick[:]), b_sb[n][:], ALU.mult)
            nc.sync.dma_start(out=out[128 * n : 128 * (n + 1), :], in_=res[:])
